import numpy as np, ml_dtypes
CORES = [68,69,70,71,76,77,78,79,84,85,86,87]
N = 12
def setup_inputs(rng):
    return {"x": rng.standard_normal((N, 128, 128), dtype=np.float32).astype(ml_dtypes.bfloat16)}
def reference(x):
    s = x.sum(axis=0, dtype=np.float64).astype(x.dtype)
    return {"y": np.broadcast_to(s, (N,) + s.shape)}

@@ -1,0 +1,132 @@
+from concourse.bass import DstId, RemoteDMATransfer
+
+SIM_CORES = 96
+S = 4
+W = 128 // S
+
+SCRATCH = {
+    "xs": ("dram", [S, 128, W], "bfloat16"),
+    "gat": ("dram", [4, 128, W], "bfloat16"),
+    "par": ("dram", [3, 128, W], "bfloat16"),
+    "res": ("dram", [S, 128, W], "bfloat16"),
+}
+SEMAPHORES = ["loaded", "sent", "arr1", "arr2", "arr3", "stored"]
+
+
+def _bits(mask):
+    return [e for e in range(mask.bit_length()) if (mask >> e) & 1]
+
+
+def _mask_of(engines):
+    m = 0
+    for e in engines:
+        m |= 1 << e
+    return m
+
+
+def _share(src, dsts, topo):
+    far = [d for d in dsts if topo.chip(d) != topo.chip(src)]
+    near = [d for d in dsts if topo.chip(d) == topo.chip(src)]
+    out = {}
+    used = []
+    for group in (far, near):
+        if not group:
+            continue
+        pool = None
+        for d in group:
+            b = set(_bits(topo.mask(src, d)))
+            pool = b if pool is None else pool & b
+        pool = sorted(pool - set(used))
+        n = 1
+        while n * 2 * len(group) <= len(pool):
+            n *= 2
+        for i, d in enumerate(group):
+            eng = pool[i * n:(i + 1) * n]
+            out[d] = (_mask_of(eng), n)
+            used += eng
+    return out
+
+
+def _plan(T, topo):
+    chips = sorted({topo.chip(r) for r in T.cores})
+    ranks, fin, agg = {}, {}, {}
+    for c in chips:
+        on = [k for k in range(SIM_CORES) if topo.chip(k) == c]
+        ranks[c] = [r for r in T.cores if topo.chip(r) == c]
+        fin[c] = [k for k in on if T.rank_of(k) is None][:S]
+    everyfin = [f for c in chips for f in fin[c]]
+    for c in chips:
+        on = [k for k in range(SIM_CORES) if topo.chip(k) == c]
+        cand = [k for k in on if all(topo.may_write(k, f) for f in everyfin if f != k)][:S]
+        while any(cand[q] == fin[c][q] for q in range(S)):
+            cand = cand[1:] + cand[:1]
+        agg[c] = cand
+    return chips, ranks, fin, agg
+
+
+def _dst(core, topo):
+    rid, pid, _ = topo.addr(core)
+    return DstId(rid=rid, pnc=pid)
+
+
+def rank_program(g, core, T, topo):
+    chips, ranks, fin, agg = _plan(T, topo)
+    c = topo.chip(core)
+    if c not in chips:
+        return
+    sem = T.sem
+    is_rank = T.rank_of(core) is not None
+    sent = 0
+
+    def step1_dsts(r):
+        return [a for a in agg[topo.chip(r)] if a != r]
+
+    def step2_dsts(q):
+        return [fin[c2][q] for c2 in chips]
+
+    if is_rank:
+        j = ranks[c].index(core)
+        g.sync.dma_start(T.xs[:], T.x[:]).then_inc(sem.loaded, 16)
+        g.wait_ge(sem.loaded, 16)
+        sh = _share(core, step1_dsts(core), topo)
+        trs = []
+        for q in range(S):
+            a = agg[c][q]
+            if a == core:
+                continue
+            trs.append(RemoteDMATransfer(dst_ids=[_dst(a, topo)], dma_engine_mask=sh[a][0], remote_sem=sem.arr1,
+                                         src=T.xs[q], dst=T.gat[j], alu_op=0))
+            sent += sh[a][1]
+        g.remote_dma_fused(trs, local_sem=sem.sent)
+
+    if core in agg[c]:
+        q = agg[c].index(core)
+        g.wait_ge(sem.arr1, sum(_share(r, step1_dsts(r), topo)[core][1] for r in ranks[c] if r != core))
+        srcs = [T.xs[q] if r == core else T.gat[jj] for jj, r in enumerate(ranks[c])]
+        sh = _share(core, step2_dsts(q), topo)
+        trs = []
+        for f in step2_dsts(q):
+            trs.append(RemoteDMATransfer(dst_ids=[_dst(f, topo)], dma_engine_mask=sh[f][0], remote_sem=sem.arr2,
+                                         srcs=srcs, dsts=[T.par[chips.index(c)]], alu_op=1))
+            sent += sh[f][1]
+        g.remote_dma_fused(trs, local_sem=sem.sent)
+
+    if core in fin[c]:
+        q = fin[c].index(core)
+        g.wait_ge(sem.arr2, sum(_share(agg[c2][q], step2_dsts(q), topo)[core][1] for c2 in chips))
+        srcs = [T.par[i] for i in range(len(chips))]
+        sh = _share(core, ranks[c], topo)
+        trs = []
+        for r in ranks[c]:
+            trs.append(RemoteDMATransfer(dst_ids=[_dst(r, topo)], dma_engine_mask=sh[r][0], remote_sem=sem.arr3,
+                                         srcs=srcs, dsts=[T.res[q]], alu_op=1))
+            sent += sh[r][1]
+        g.remote_dma_fused(trs, local_sem=sem.sent)
+
+    if is_rank:
+        g.sync.wait_ge(sem.arr3, sum(_share(f, ranks[c], topo)[core][1] for f in fin[c]))
+        g.sync.dma_start(T.y[:], T.res[:]).then_inc(sem.stored, 16)
+        g.sync.wait_ge(sem.stored, 16)
+
+    if sent:
+        g.wait_ge(sem.sent, sent)

@@ -24,27 +24,42 @@ def _mask_of(engines):
     return m
 
 
-def _share(src, dsts, topo):
+def _pool(src, group, used, topo):
+    pool = None
+    for d in group:
+        b = set(_bits(topo.mask(src, d)))
+        pool = b if pool is None else pool & b
+    return sorted(pool - set(used))
+
+
+def _pow2(n):
+    p = 1
+    while p * 2 <= n:
+        p *= 2
+    return p
+
+
+def _each(src, dsts, topo):
+    pool = _pool(src, dsts, [], topo)
+    n = _pow2(len(pool) // len(dsts))
+    return {d: (_mask_of(pool[i * n:(i + 1) * n]), n) for i, d in enumerate(dsts)}
+
+
+def _groups(src, dsts, topo):
     far = [d for d in dsts if topo.chip(d) != topo.chip(src)]
     near = [d for d in dsts if topo.chip(d) == topo.chip(src)]
-    out = {}
-    used = []
+    out, used = [], []
     for group in (far, near):
-        if not group:
-            continue
-        pool = None
-        for d in group:
-            b = set(_bits(topo.mask(src, d)))
-            pool = b if pool is None else pool & b
-        pool = sorted(pool - set(used))
-        n = 1
-        while n * 2 * len(group) <= len(pool):
-            n *= 2
-        for i, d in enumerate(group):
-            eng = pool[i * n:(i + 1) * n]
-            out[d] = (_mask_of(eng), n)
+        if group:
+            pool = _pool(src, group, used, topo)
+            eng = pool[:_pow2(len(pool))]
+            out.append((group, _mask_of(eng), len(eng)))
             used += eng
     return out
+
+
+def _lands(src, dsts, dst, topo):
+    return sum(n for group, _, n in _groups(src, dsts, topo) if dst in group)
 
 
 def _plan(T, topo):
@@ -84,11 +99,20 @@ def rank_program(g, core, T, topo):
     def step2_dsts(q):
         return [fin[c2][q] for c2 in chips]
 
+    def fold(srcs, dsts, out_ap, remote_sem):
+        trs, n_all = [], 0
+        for group, mask, n in _groups(core, dsts, topo):
+            trs.append(RemoteDMATransfer(dst_ids=[_dst(d, topo) for d in group], dma_engine_mask=mask,
+                                         remote_sem=remote_sem, srcs=srcs, dsts=[out_ap for d in group], alu_op=1))
+            n_all += n
+        g.remote_dma_fused(trs, local_sem=sem.sent)
+        return n_all
+
     if is_rank:
         j = ranks[c].index(core)
         g.sync.dma_start(T.xs[:], T.x[:]).then_inc(sem.loaded, 16)
         g.wait_ge(sem.loaded, 16)
-        sh = _share(core, step1_dsts(core), topo)
+        sh = _each(core, step1_dsts(core), topo)
         trs = []
         for q in range(S):
             a = agg[c][q]
@@ -101,30 +125,17 @@ def rank_program(g, core, T, topo):
 
     if core in agg[c]:
         q = agg[c].index(core)
-        g.wait_ge(sem.arr1, sum(_share(r, step1_dsts(r), topo)[core][1] for r in ranks[c] if r != core))
+        g.wait_ge(sem.arr1, sum(_each(r, step1_dsts(r), topo)[core][1] for r in ranks[c] if r != core))
         srcs = [T.xs[q] if r == core else T.gat[jj] for jj, r in enumerate(ranks[c])]
-        sh = _share(core, step2_dsts(q), topo)
-        trs = []
-        for f in step2_dsts(q):
-            trs.append(RemoteDMATransfer(dst_ids=[_dst(f, topo)], dma_engine_mask=sh[f][0], remote_sem=sem.arr2,
-                                         srcs=srcs, dsts=[T.par[chips.index(c)]], alu_op=1))
-            sent += sh[f][1]
-        g.remote_dma_fused(trs, local_sem=sem.sent)
+        sent += fold(srcs, step2_dsts(q), T.par[chips.index(c)], sem.arr2)
 
     if core in fin[c]:
         q = fin[c].index(core)
-        g.wait_ge(sem.arr2, sum(_share(agg[c2][q], step2_dsts(q), topo)[core][1] for c2 in chips))
-        srcs = [T.par[i] for i in range(len(chips))]
-        sh = _share(core, ranks[c], topo)
-        trs = []
-        for r in ranks[c]:
-            trs.append(RemoteDMATransfer(dst_ids=[_dst(r, topo)], dma_engine_mask=sh[r][0], remote_sem=sem.arr3,
-                                         srcs=srcs, dsts=[T.res[q]], alu_op=1))
-            sent += sh[r][1]
-        g.remote_dma_fused(trs, local_sem=sem.sent)
+        g.wait_ge(sem.arr2, sum(_lands(agg[c2][q], step2_dsts(q), core, topo) for c2 in chips))
+        sent += fold([T.par[i] for i in range(len(chips))], ranks[c], T.res[q], sem.arr3)
 
     if is_rank:
-        g.sync.wait_ge(sem.arr3, sum(_share(f, ranks[c], topo)[core][1] for f in fin[c]))
+        g.sync.wait_ge(sem.arr3, sum(_lands(f, ranks[c], core, topo) for f in fin[c]))
         g.sync.dma_start(T.y[:], T.res[:]).then_inc(sem.stored, 16)
         g.sync.wait_ge(sem.stored, 16)
 

@@ -24,12 +24,12 @@ def _mask_of(engines):
     return m
 
 
-def _pool(src, group, used, topo):
+def _pool(src, group, topo):
     pool = None
     for d in group:
         b = set(_bits(topo.mask(src, d)))
         pool = b if pool is None else pool & b
-    return sorted(pool - set(used))
+    return sorted(pool)
 
 
 def _pow2(n):
@@ -40,26 +40,22 @@ def _pow2(n):
 
 
 def _each(src, dsts, topo):
-    pool = _pool(src, dsts, [], topo)
+    pool = _pool(src, dsts, topo)
     n = _pow2(len(pool) // len(dsts))
     return {d: (_mask_of(pool[i * n:(i + 1) * n]), n) for i, d in enumerate(dsts)}
 
 
-def _groups(src, dsts, topo):
-    far = [d for d in dsts if topo.chip(d) != topo.chip(src)]
-    near = [d for d in dsts if topo.chip(d) == topo.chip(src)]
-    out, used = [], []
-    for group in (far, near):
-        if group:
-            pool = _pool(src, group, used, topo)
-            eng = pool[:_pow2(len(pool))]
-            out.append((group, _mask_of(eng), len(eng)))
-            used += eng
-    return out
+def _hops(src, dst, topo):
+    a, b = topo.chip(src), topo.chip(dst)
+    if a == b:
+        return 0
+    return 1 if topo.mates(a, b) or topo.same_plane(a, b) else 2
 
 
-def _lands(src, dsts, dst, topo):
-    return sum(n for group, _, n in _groups(src, dsts, topo) if dst in group)
+def _all(src, dsts, topo):
+    pool = _pool(src, dsts, topo)
+    eng = pool[:_pow2(len(pool))]
+    return sorted(dsts, key=lambda d: -_hops(src, d, topo)), _mask_of(eng), len(eng)
 
 
 def _plan(T, topo):
@@ -100,13 +96,11 @@ def rank_program(g, core, T, topo):
         return [fin[c2][q] for c2 in chips]
 
     def fold(srcs, dsts, out_ap, remote_sem):
-        trs, n_all = [], 0
-        for group, mask, n in _groups(core, dsts, topo):
-            trs.append(RemoteDMATransfer(dst_ids=[_dst(d, topo) for d in group], dma_engine_mask=mask,
-                                         remote_sem=remote_sem, srcs=srcs, dsts=[out_ap for d in group], alu_op=1))
-            n_all += n
-        g.remote_dma_fused(trs, local_sem=sem.sent)
-        return n_all
+        order, mask, n = _all(core, dsts, topo)
+        g.remote_dma_fused([RemoteDMATransfer(dst_ids=[_dst(d, topo) for d in order], dma_engine_mask=mask,
+                                              remote_sem=remote_sem, srcs=srcs, dsts=[out_ap for d in order],
+                                              alu_op=1)], local_sem=sem.sent)
+        return n
 
     if is_rank:
         j = ranks[c].index(core)
@@ -131,11 +125,11 @@ def rank_program(g, core, T, topo):
 
     if core in fin[c]:
         q = fin[c].index(core)
-        g.wait_ge(sem.arr2, sum(_lands(agg[c2][q], step2_dsts(q), core, topo) for c2 in chips))
+        g.wait_ge(sem.arr2, sum(_all(agg[c2][q], step2_dsts(q), topo)[2] for c2 in chips))
         sent += fold([T.par[i] for i in range(len(chips))], ranks[c], T.res[q], sem.arr3)
 
     if is_rank:
-        g.sync.wait_ge(sem.arr3, sum(_lands(f, ranks[c], core, topo) for f in fin[c]))
+        g.sync.wait_ge(sem.arr3, sum(_all(f, ranks[c], topo)[2] for f in fin[c]))
         g.sync.dma_start(T.y[:], T.res[:]).then_inc(sem.stored, 16)
         g.sync.wait_ge(sem.stored, 16)
 

from concourse.bass import DstId, RemoteDMATransfer

SIM_CORES = 96
S = 4
W = 128 // S

SCRATCH = {
    "xs": ("dram", [S, 128, W], "bfloat16"),
    "gat": ("dram", [4, 128, W], "bfloat16"),
    "par": ("dram", [3, 128, W], "bfloat16"),
    "res": ("dram", [S, 128, W], "bfloat16"),
}
SEMAPHORES = ["loaded", "sent", "arr1", "arr2", "arr3", "stored"]


def _bits(mask):
    return [e for e in range(mask.bit_length()) if (mask >> e) & 1]


def _mask_of(engines):
    m = 0
    for e in engines:
        m |= 1 << e
    return m


def _pool(src, group, topo):
    pool = None
    for d in group:
        b = set(_bits(topo.mask(src, d)))
        pool = b if pool is None else pool & b
    return sorted(pool)


def _pow2(n):
    p = 1
    while p * 2 <= n:
        p *= 2
    return p


def _each(src, dsts, topo):
    pool = _pool(src, dsts, topo)
    n = _pow2(len(pool) // len(dsts))
    return {d: (_mask_of(pool[i * n:(i + 1) * n]), n) for i, d in enumerate(dsts)}


def _hops(src, dst, topo):
    a, b = topo.chip(src), topo.chip(dst)
    if a == b:
        return 0
    return 1 if topo.mates(a, b) or topo.same_plane(a, b) else 2


def _all(src, dsts, topo):
    pool = _pool(src, dsts, topo)
    eng = pool[:_pow2(len(pool))]
    return sorted(dsts, key=lambda d: -_hops(src, d, topo)), _mask_of(eng), len(eng)


def _plan(T, topo):
    chips = sorted({topo.chip(r) for r in T.cores})
    ranks, fin, agg = {}, {}, {}
    for c in chips:
        on = [k for k in range(SIM_CORES) if topo.chip(k) == c]
        ranks[c] = [r for r in T.cores if topo.chip(r) == c]
        fin[c] = [k for k in on if T.rank_of(k) is None][:S]
    everyfin = [f for c in chips for f in fin[c]]
    for c in chips:
        on = [k for k in range(SIM_CORES) if topo.chip(k) == c]
        cand = [k for k in on if all(topo.may_write(k, f) for f in everyfin if f != k)][:S]
        while any(cand[q] == fin[c][q] for q in range(S)):
            cand = cand[1:] + cand[:1]
        agg[c] = cand
    return chips, ranks, fin, agg


def _dst(core, topo):
    rid, pid, _ = topo.addr(core)
    return DstId(rid=rid, pnc=pid)


def rank_program(g, core, T, topo):
    chips, ranks, fin, agg = _plan(T, topo)
    c = topo.chip(core)
    if c not in chips:
        return
    sem = T.sem
    is_rank = T.rank_of(core) is not None
    sent = 0

    def step1_dsts(r):
        return [a for a in agg[topo.chip(r)] if a != r]

    def step2_dsts(q):
        return [fin[c2][q] for c2 in chips]

    def fold(srcs, dsts, out_ap, remote_sem):
        order, mask, n = _all(core, dsts, topo)
        g.remote_dma_fused([RemoteDMATransfer(dst_ids=[_dst(d, topo) for d in order], dma_engine_mask=mask,
                                              remote_sem=remote_sem, srcs=srcs, dsts=[out_ap for d in order],
                                              alu_op=1)], local_sem=sem.sent)
        return n

    if is_rank:
        j = ranks[c].index(core)
        g.sync.dma_start(T.xs[:], T.x[:]).then_inc(sem.loaded, 16)
        g.wait_ge(sem.loaded, 16)
        sh = _each(core, step1_dsts(core), topo)
        trs = []
        for q in range(S):
            a = agg[c][q]
            if a == core:
                continue
            trs.append(RemoteDMATransfer(dst_ids=[_dst(a, topo)], dma_engine_mask=sh[a][0], remote_sem=sem.arr1,
                                         src=T.xs[q], dst=T.gat[j], alu_op=0))
            sent += sh[a][1]
        g.remote_dma_fused(trs, local_sem=sem.sent)

    if core in agg[c]:
        q = agg[c].index(core)
        g.wait_ge(sem.arr1, sum(_each(r, step1_dsts(r), topo)[core][1] for r in ranks[c] if r != core))
        srcs = [T.xs[q] if r == core else T.gat[jj] for jj, r in enumerate(ranks[c])]
        sent += fold(srcs, step2_dsts(q), T.par[chips.index(c)], sem.arr2)

    if core in fin[c]:
        q = fin[c].index(core)
        g.wait_ge(sem.arr2, sum(_all(agg[c2][q], step2_dsts(q), topo)[2] for c2 in chips))
        sent += fold([T.par[i] for i in range(len(chips))], ranks[c], T.res[q], sem.arr3)

    if is_rank:
        g.sync.wait_ge(sem.arr3, sum(_all(f, ranks[c], topo)[2] for f in fin[c]))
        g.sync.dma_start(T.y[:], T.res[:]).then_inc(sem.stored, 16)
        g.sync.wait_ge(sem.stored, 16)

    if sent:
        g.wait_ge(sem.sent, sent)
